import numpy as np
import ml_dtypes


def mxq(x, axis, fmt="e4m3"):
    dtype, down = {"e4m3": (ml_dtypes.float8_e4m3fn, 7), "e5m2": (ml_dtypes.float8_e5m2, 14)}[fmt]
    v = np.moveaxis(np.asarray(x, np.float32).astype(ml_dtypes.bfloat16).astype(np.float64), axis, -1)
    blocks = v.reshape(v.shape[:-1] + (-1, 32))
    amax = np.abs(blocks).max(-1, keepdims=True)
    byte = np.maximum(np.where(amax > 0, np.frexp(amax)[1] - 1 + 127, 0) - down, 1)
    scale = np.exp2(byte - 127.0)
    codes = (blocks / scale).astype(np.float32).astype(dtype).astype(np.float64)
    return np.moveaxis((codes * scale).reshape(v.shape), -1, axis)


WIDE = False


def mx_kscale(k):
    if not WIDE:
        return np.ones(k)
    levels = np.array([10, -10, 5, -5, 0])
    if k % 512:
        return np.exp2(np.random.permutation(np.resize(levels, k // 32))).repeat(32)
    a = np.empty((k // 512, 16))
    for p in range(k // 512):
        a[p, :8] = np.random.permutation(np.resize(levels, 8))
        for g in range(8):
            far = levels[np.abs(levels - a[p, g]) >= 10]
            a[p, g + 8] = far[np.random.randint(len(far))]
    return np.exp2(a.ravel()).repeat(32)


def f64(x):
    return np.asarray(x).astype(np.float64)


def striped(idx):
    return np.tile(idx.reshape(-1, 16).T, (8, 1)).astype(np.uint16)


def unstriped(offs):
    return offs[:16].T.reshape(-1).astype(np.int64)


def striped8(idx):
    return np.concatenate([x.reshape(-1, 16).T for x in idx]).astype(np.uint16)


def runs(offs, k):
    lists = np.stack([offs[16 * r : 16 * r + 16].T.reshape(-1) for r in range(8)]).astype(np.int64)
    return lists[np.arange(k) % 512 // 64]


def pack_weight(w):
    k, n = w.shape
    w = f64(np.asarray(w, np.float32).astype(ml_dtypes.bfloat16)).reshape(k // 32, 32, n)
    amax = np.abs(w).max(1)
    byte = np.clip(np.where(amax > 0, np.frexp(amax)[1] - 1 + 127 - 7, 1), 1, 254)
    scaled = (w * np.exp2(127.0 - byte)[:, None, :]).reshape(k, n).astype(np.float32)
    words = np.ascontiguousarray(scaled.reshape(k // 512, 128, 4, n).transpose(0, 1, 3, 2)).astype(ml_dtypes.float8_e4m3fn).view(np.uint8)
    return words, np.ascontiguousarray(byte.astype(np.uint8).reshape(k // 512, 16, n))


def unpack_weight(words, scales):
    g, p, n, _ = words.shape
    vals = np.ascontiguousarray(words).view(ml_dtypes.float8_e4m3fn).astype(np.float64) * np.repeat(np.exp2(scales.astype(np.float64) - 127.0), 8, axis=1)[..., None]
    return vals.transpose(0, 1, 3, 2).reshape(g * 512, n)


def sigmoid(v):
    return 1.0 / (1.0 + np.exp(-np.maximum(v, -700.0)))

def planes(y):
    n, m = y.shape
    v = y.astype(np.float32).astype(ml_dtypes.bfloat16).astype(np.float64).reshape(n // 32, 32, m)
    top = np.abs(v).max(1)
    byte = np.clip(np.where(top > 0, np.frexp(top)[1] - 1 + 127 - 7, 1), 1, 254)
    codes = (v * np.exp2(127.0 - byte)[:, None, :]).reshape(n, m).astype(np.float32).astype(ml_dtypes.float8_e4m3fn).view(np.uint8)
    words = codes.reshape(n // 512, 128, 4, m).transpose(0, 1, 3, 2)
    return np.ascontiguousarray(words), np.ascontiguousarray(byte.astype(np.uint8).reshape(n // 512, 16, m))


K, T, S, G, H, W, C = 512, 1024, 512, 2048, 512, 384, 512


def setup_inputs():
    n = np.random.standard_normal
    s = mx_kscale(K)[:, None]
    packed_xT = pack_weight(n((K, T)) * s)
    packed_dT = pack_weight(n((K, G)) / s)
    return {
        "x_words": packed_xT[0],
        "x_scales": packed_xT[1],
        "d_words": packed_dT[0],
        "d_scales": packed_dT[1],
        "gs": (np.random.uniform(0.5, 1.5, (K, 1)) / s).astype(np.float32),
        "tau": np.random.uniform(0.3, 0.9, (C, 1)).astype(np.float32),
        "offs": striped(np.random.permutation(T)[:S]),
        "k1": striped8(np.random.randint(0, G, (8, H))),
        "n1": striped(np.random.permutation(S)[:W]),
        "n2": striped(np.random.permutation(S)[:W]),
        "cand": striped(np.random.permutation(T)[:C]),
        "n3": striped(np.random.randint(0, S, G)),
    }


def reference(x_words, x_scales, d_words, d_scales, gs, tau, offs, k1, n1, n2, cand, n3):
    x_cand = unpack_weight(x_words, x_scales)[:, unstriped(cand)]
    d_k1 = unpack_weight(d_words, d_scales)[np.arange(K)[:, None], runs(k1, K)]
    xq = unpack_weight(x_words, x_scales)[:, unstriped(offs)]
    h = 0.0625 * (d_k1.T @ xq)
    old = h[:, unstriped(n1)]
    pa = h[:, unstriped(n2)]
    ra = old * sigmoid(pa)
    ds = h.copy()
    ds[:, unstriped(n1)] = ra
    z = f64(gs) * ds
    s = 0.0625 * ((x_cand.T @ mxq(z, 0, "e4m3")))
    top = s.max(axis=1, keepdims=True)
    ea = np.exp(f64(tau) * (s[:, unstriped(n3)] - top))
    mx = ea.reshape(C, S, 4).max(axis=2)
    mn = ea.reshape(C, S, 4).min(axis=2)
    out_0 = 3.0 * (s * (mx - mn))
    return (out_0,) + planes(out_0)

@@ -1,0 +1,280 @@
+from contextlib import ExitStack
+
+import concourse.mybir as mybir
+
+K, T, S, G, H, W, C = 512, 1024, 512, 2048, 512, 384, 512
+FLOPS = 2 * K * H * S + 2 * K * C * S
+
+F32 = mybir.dt.float32
+BF16 = mybir.dt.bfloat16
+I32 = mybir.dt.int32
+U32 = mybir.dt.uint32
+U16 = mybir.dt.uint16
+U8 = mybir.dt.uint8
+FP8X4 = mybir.dt.float8_e4m3fn_x4
+ALU = mybir.AluOpType
+ACT = mybir.ActivationFunctionType
+
+P = 128
+PACK = 4
+MEMBERS = 4
+HALF = S // 2
+CHUNK = 128
+WINDOW = 1024
+GRANULES = [(c, ts) for c in range(S // CHUNK) for ts in ((0, 1), (2, 3))]
+
+
+def tile_picked_pqckgateegp_none_po_kernel(
+    tc, x_words, x_scales, d_words, d_scales, gs, tau, offs, k1, n1, n2, cand, n3, out_0, out_1, out_2
+):
+    nc = tc.nc
+    with ExitStack() as ctx:
+        pool = ctx.enter_context(tc.tile_pool(name="sbuf", bufs=1))
+        psum = ctx.enter_context(tc.psum_pool(name="psum", bufs=1))
+
+        def sb(name, shape, dtype, tag=None):
+            return pool.tile(shape, dtype, name=name, tag=tag or name, align_bytes=64)
+
+        def load_list(name, src):
+            tile = sb(name, list(src.shape), U16)
+            nc.sync.dma_start(tile[:], src)
+            return tile
+
+        def deal(dst, src):
+            nc.vector.tensor_copy(
+                out=dst[:].rearrange("p (t m) -> p t m", t=PACK), in_=src[:].rearrange("p (m t) -> p t m", t=PACK)
+            )
+
+        d_table_bytes = sb("d_table_bytes", [P, G], U8)
+        x_table_bytes = sb("x_table_bytes", [P, T], U8)
+        nc.vector.memset(x_table_bytes[:].bitcast(I32), 0)
+
+        k1_list = load_list("k1_list", k1)
+        d_table_words = sb("d_table_words", [P, G], U32)
+        nc.scalar.dma_start(d_table_words[:].bitcast(I32), d_words[0].rearrange("p n t -> p (n t)").bitcast(I32))
+        x_table_words = sb("x_table_words", [P, T], U32)
+        nc.scalar.dma_start(x_table_words[:].bitcast(I32), x_words[0].rearrange("p n t -> p (n t)").bitcast(I32))
+        d_rows = d_scales[0].bitcast(I32).rearrange("(r j) c -> j r c", j=2)
+        for j in range(2):
+            nc.sync.dma_start(
+                d_table_bytes[j:P:2, :].bitcast(I32), d_rows[j].unsqueeze(1).to_broadcast([8, 8, G // 4])
+            )
+        offs_list = load_list("offs_list", offs)
+        x_rows = x_scales[0].bitcast(I32)
+        for q in range(4):
+            nc.sync.dma_start(x_table_bytes[32 * q : 32 * q + 4, :].bitcast(I32), x_rows[4 * q : 4 * q + 4, :])
+        n1_list = load_list("n1_list", n1)
+        n2_list = load_list("n2_list", n2)
+        cand_list = load_list("cand_list", cand)
+        n3_list = load_list("n3_list", n3)
+        gs_sb = sb("gs_sb", [P, PACK], F32)
+        tau_sb = sb("tau_sb", [P, PACK], F32)
+        nc.gpsimd.dma_start(gs_sb[:], gs.rearrange("(p t) o -> p (t o)", t=PACK))
+        nc.gpsimd.dma_start(tau_sb[:], tau.rearrange("(p t) o -> p (t o)", t=PACK))
+
+        s_rows = [sb(f"s_rows{t}", [P, WINDOW], F32) for t in range(PACK)]
+        for t in range(PACK):
+            nc.vector.memset(s_rows[t][:, S:WINDOW], 0.0)
+
+        d_bytes = sb("d_bytes", [P, H], U8)
+        nc.vector.tensor_copy(out=d_bytes[:], in_=d_table_bytes[:].indirect(k1_list[:]))
+        d_plane = sb("d_plane", [P, H], U8, tag="stationary_plane")
+        deal(d_plane, d_bytes)
+        for j in range(2):
+            nc.scalar.dma_start(d_plane[2 + j : P : 32, :].bitcast(I32), d_plane[16 + j : P : 32, :].bitcast(I32))
+        d_picked = sb("d_picked", [P, H], U32)
+        nc.vector.tensor_copy(out=d_picked[:], in_=d_table_words[:].indirect(k1_list[:]))
+        d_codes = sb("d_codes", [P, H], U32, tag="stationary_codes")
+        deal(d_codes, d_picked)
+
+        xq_codes = [sb(f"xq_codes{u}", [P, HALF], U32) for u in range(2)]
+        xq_plane = [sb(f"xq_plane{u}", [P, HALF], U8) for u in range(2)]
+        for u in range(2):
+            picks = offs_list[:, u * HALF // 16 : (u + 1) * HALF // 16]
+            nc.vector.tensor_copy(out=xq_codes[u][:], in_=x_table_words[:].indirect(picks))
+            nc.vector.tensor_copy(out=xq_plane[u][:], in_=x_table_bytes[:].indirect(picks))
+
+        neg_tau = sb("neg_tau", [P, PACK], F32)
+        nc.vector.tensor_scalar(neg_tau[:], tau_sb[:], -1.0, None, ALU.mult)
+
+        h_rows = [sb(f"h_rows{t}", [P, S], F32) for t in range(PACK)]
+        h_banks = {}
+        for u in range(2):
+            for t in range(PACK):
+                cols = slice(t * P, (t + 1) * P)
+                h_banks[t, u] = psum.tile([P, HALF], F32, name=f"h_bank{t}_{u}", tag=f"bank{t}_{u}")
+                nc.tensor.matmul_mx(
+                    out=h_banks[t, u][:],
+                    lhsT=d_codes[:, cols].bitcast(FP8X4),
+                    lhsT_scale=d_plane[:, cols],
+                    rhs=xq_codes[u][:].bitcast(FP8X4),
+                    rhs_scale=xq_plane[u][:],
+                    start=True,
+                    stop=True,
+                )
+        for t in range(PACK):
+            nc.scalar.activation(h_rows[t][:, 0:HALF], h_banks[t, 0][:], ACT.Copy, scale=0.0625)
+
+        ds_rows = [sb(f"ds_rows{t}", [P, S], F32) for t in range(PACK)]
+        half_old = [sb(f"half_old{t}", [P, W], F32) for t in range(PACK)]
+        pa = [sb(f"pa{t}", [P, W], F32) for t in range(PACK)]
+        gate = [sb(f"gate{t}", [P, W], F32) for t in range(PACK)]
+        ra = [sb(f"ra{t}", [P, W], F32) for t in range(PACK)]
+
+        def finish_h(t):
+            nc.vector.tensor_scalar(h_rows[t][:, HALF:S], h_banks[t, 1][:], 0.0625, None, ALU.mult)
+            nc.scalar.activation(half_old[t][:], h_rows[t][:].indirect(n1_list[:]), ACT.Copy, scale=0.5)
+
+        def fetch_gate(t):
+            nc.vector.tensor_copy(out=pa[t][:], in_=h_rows[t][:].indirect(n2_list[:]))
+            nc.scalar.activation(gate[t][:], pa[t][:], ACT.Tanh, scale=0.5)
+
+        def gated(t):
+            nc.vector.tensor_copy(out=ds_rows[t][:], in_=h_rows[t][:])
+            nc.vector.scalar_tensor_tensor(ra[t][:], gate[t][:], 1.0, half_old[t][:], ALU.add, ALU.mult)
+
+        def put_back(t):
+            nc.scalar.activation(ds_rows[t][:].indirect(n1_list[:]), ra[t][:], ACT.Copy)
+
+        finish_h(0)
+        fetch_gate(0)
+        finish_h(1)
+        gated(0)
+        put_back(0)
+        fetch_gate(1)
+        for t in range(2, PACK):
+            finish_h(t)
+        for t in range(2, PACK):
+            fetch_gate(t)
+        for t in range(1, PACK):
+            gated(t)
+        for t in range(1, PACK):
+            put_back(t)
+
+        cand_picked = sb("cand_picked", [P, C], U32, tag="stationary_codes")
+        cand_bytes = sb("cand_bytes", [P, C], U8, tag="stationary_plane")
+        cand_codes = sb("cand_codes", [P, C], U32)
+        cand_plane = sb("cand_plane", [P, C], U8)
+        nc.vector.tensor_copy(out=cand_picked[:], in_=x_table_words[:].indirect(cand_list[:]))
+        nc.vector.tensor_copy(out=cand_bytes[:], in_=x_table_bytes[:].indirect(cand_list[:]))
+        deal(cand_codes, cand_picked)
+        deal(cand_plane, cand_bytes)
+
+        z_bf = [sb(f"z_bf{u}", [P, HALF, PACK], BF16) for u in range(2)]
+        z_codes = [sb(f"z_codes{u}", [P, HALF], U32) for u in range(2)]
+        z_plane = [sb(f"z_plane{u}", [P, HALF], U8) for u in range(2)]
+        for t in range(PACK):
+            for u in range(2):
+                nc.vector.tensor_scalar(
+                    z_bf[u][:, :, t], ds_rows[t][:, u * HALF : (u + 1) * HALF], gs_sb[:, t : t + 1], None, ALU.mult
+                )
+        for u in range(2):
+            nc.vector.quantize_mx(
+                out=z_codes[u][:].bitcast(FP8X4), scales=z_plane[u][:], in_=z_bf[u][:].rearrange("p j t -> p (j t)")
+            )
+
+        bias = []
+        for t in range(PACK):
+            cols = slice(t * P, (t + 1) * P)
+            s_bank = psum.tile([P, S], F32, name=f"s_bank{t}", tag=f"bank{t}_0")
+            for u in range(2):
+                nc.tensor.matmul_mx(
+                    out=s_bank[:, u * HALF : (u + 1) * HALF],
+                    lhsT=cand_codes[:, cols].bitcast(FP8X4),
+                    lhsT_scale=cand_plane[:, cols],
+                    rhs=z_codes[u][:].bitcast(FP8X4),
+                    rhs_scale=z_plane[u][:],
+                    start=True,
+                    stop=True,
+                )
+            top = sb(f"top{t}", [P, 1], F32)
+            nc.vector.tensor_scalar(s_rows[t][:, 0:S], s_bank[:], 0.0625, None, ALU.mult, ALU.max, accum_out=top[:])
+            bias.append(sb(f"bias{t}", [P, 1], F32))
+            nc.scalar.activation(bias[t][:], top[:], ACT.Copy, scale=neg_tau[:, t : t + 1])
+
+        entries = CHUNK * MEMBERS
+        ea = []
+        for g, (c, ts) in enumerate(GRANULES):
+            ea.append(sb(f"ea{g}", [P, len(ts) * entries], F32))
+            picks = n3_list[:, c * entries // 16 : (c + 1) * entries // 16]
+            for i, t in enumerate(ts):
+                nc.scalar.activation(
+                    ea[g][:, i * entries : (i + 1) * entries],
+                    s_rows[t][:].indirect(picks),
+                    ACT.Exp,
+                    bias=bias[t][:],
+                    scale=tau_sb[:, t : t + 1],
+                )
+
+        out_chunks = [sb(f"out_chunk{c}", [P, PACK, CHUNK], F32) for c in range(S // CHUNK)]
+        out_rows = out_0.rearrange("(p t) j -> p t j", t=PACK)
+        hi, lo, mx, mn, spread = {}, {}, {}, {}, {}
+
+        def pairs(g, store, name, op):
+            n = len(GRANULES[g][1]) * CHUNK
+            store[g] = sb(f"{name}{g}", [P, n, 2], F32)
+            members = ea[g][:].rearrange("p (j m) -> p j m", m=MEMBERS)
+            nc.vector.tensor_tensor(store[g][:], members[:, :, 0:2], members[:, :, 2:4], op)
+
+        def fours(g, store, name, src, op):
+            n = len(GRANULES[g][1]) * CHUNK
+            store[g] = sb(f"{name}{g}", [P, n], F32)
+            nc.vector.tensor_tensor(store[g][:], src[g][:, :, 0], src[g][:, :, 1], op)
+
+        def difference(g):
+            n = len(GRANULES[g][1]) * CHUNK
+            spread[g] = sb(f"spread{g}", [P, n], F32)
+            nc.vector.tensor_tensor(spread[g][:], mx[g][:], mn[g][:], ALU.subtract)
+
+        def result(g):
+            c, ts = GRANULES[g]
+            for i, t in enumerate(ts):
+                nc.vector.scalar_tensor_tensor(
+                    out_chunks[c][:, t, :],
+                    spread[g][:, i * CHUNK : (i + 1) * CHUNK],
+                    3.0,
+                    s_rows[t][:, c * CHUNK : (c + 1) * CHUNK],
+                    ALU.mult,
+                    ALU.mult,
+                )
+            if ts[-1] == PACK - 1:
+                nc.sync.dma_start(out_rows[:, :, c * CHUNK : (c + 1) * CHUNK], out_chunks[c][:])
+
+        out_codes = sb("out_codes", [P, S], U32)
+        out_plane = sb("out_plane", [P, S], U8)
+        out_bf = [sb(f"out_bf{c}", [P, CHUNK, PACK], BF16) for c in range(S // CHUNK)]
+
+        def quantise(c):
+            cols = slice(c * CHUNK, (c + 1) * CHUNK)
+            nc.vector.quantize_mx(
+                out=out_codes[:, cols].bitcast(FP8X4),
+                scales=out_plane[:, cols],
+                in_=out_bf[c][:].rearrange("p j t -> p (j t)"),
+            )
+
+        last = len(GRANULES) - 1
+        for g in range(len(GRANULES)):
+            pairs(g, hi, "hi", ALU.max)
+            if g > 0:
+                difference(g - 1)
+            pairs(g, lo, "lo", ALU.min)
+            if g > 0:
+                result(g - 1)
+            fours(g, mx, "mx", hi, ALU.max)
+            fours(g, mn, "mn", lo, ALU.min)
+        last_chunk = S // CHUNK - 1
+        for c in range(last_chunk):
+            nc.scalar.activation(out_bf[c][:], out_chunks[c][:].rearrange("p t j -> p j t"), ACT.Copy)
+        quantise(0)
+        difference(last)
+        quantise(1)
+        result(last)
+        quantise(2)
+        nc.vector.tensor_copy(out=out_bf[last_chunk][:], in_=out_chunks[last_chunk][:].rearrange("p t j -> p j t"))
+        quantise(last_chunk)
+
+        nc.sync.dma_start(out_1[0].rearrange("p n t -> p (n t)").bitcast(I32), out_codes[:].bitcast(I32))
+        plane_rows = out_2[0].bitcast(I32)
+        for q in range(4):
+            queue = nc.scalar if q % 2 == 0 else nc.sync
+            queue.dma_start(plane_rows[4 * q : 4 * q + 4, :], out_plane[32 * q : 32 * q + 4, :].bitcast(I32))

@@ -19,9 +19,15 @@ P = 128
 PACK = 4
 MEMBERS = 4
 HALF = S // 2
-CHUNK = 128
 WINDOW = 1024
-GRANULES = [(c, ts) for c in range(S // CHUNK) for ts in ((0, 1), (2, 3))]
+PICKS = 512
+CHUNKS = [(0, 256), (256, 128), (384, 128)]
+GRANULE = 256
+GRANULES = [
+    (c, tuple(range(t0, t0 + GRANULE // width)))
+    for c, (start, width) in enumerate(CHUNKS)
+    for t0 in range(0, PACK, GRANULE // width)
+]
 
 
 def tile_picked_pqckgateegp_none_po_kernel(
@@ -40,52 +46,48 @@ def tile_picked_pqckgateegp_none_po_kernel(
             nc.sync.dma_start(tile[:], src)
             return tile
 
-        def deal(dst, src):
+        def deal(dst, src, run):
             nc.vector.tensor_copy(
-                out=dst[:].rearrange("p (t m) -> p t m", t=PACK), in_=src[:].rearrange("p (m t) -> p t m", t=PACK)
+                out=dst[:].rearrange("p (t b i) -> p b t i", t=PACK, i=run),
+                in_=src[:].rearrange("p (b i t) -> p b t i", t=PACK, i=run),
             )
 
         d_table_bytes = sb("d_table_bytes", [P, G], U8)
         x_table_bytes = sb("x_table_bytes", [P, T], U8)
-        nc.vector.memset(x_table_bytes[:].bitcast(I32), 0)
-
-        k1_list = load_list("k1_list", k1)
-        d_table_words = sb("d_table_words", [P, G], U32)
-        nc.scalar.dma_start(d_table_words[:].bitcast(I32), d_words[0].rearrange("p n t -> p (n t)").bitcast(I32))
-        x_table_words = sb("x_table_words", [P, T], U32)
-        nc.scalar.dma_start(x_table_words[:].bitcast(I32), x_words[0].rearrange("p n t -> p (n t)").bitcast(I32))
-        d_rows = d_scales[0].bitcast(I32).rearrange("(r j) c -> j r c", j=2)
-        for j in range(2):
-            nc.sync.dma_start(
-                d_table_bytes[j:P:2, :].bitcast(I32), d_rows[j].unsqueeze(1).to_broadcast([8, 8, G // 4])
-            )
-        offs_list = load_list("offs_list", offs)
         x_rows = x_scales[0].bitcast(I32)
         for q in range(4):
-            nc.sync.dma_start(x_table_bytes[32 * q : 32 * q + 4, :].bitcast(I32), x_rows[4 * q : 4 * q + 4, :])
+            nc.scalar.dma_start(
+                x_table_bytes[32 * q : 32 * q + 32, :].bitcast(I32),
+                x_rows[4 * q : 4 * q + 4, :].unsqueeze(0).to_broadcast([8, 4, T // 4]),
+            )
+
+        k1_list = load_list("k1_list", k1)
+        d_rows = d_scales[0].bitcast(I32)
+        nc.sync.dma_start(d_table_bytes[:].bitcast(I32), d_rows.unsqueeze(1).to_broadcast([16, 8, G // 4]))
+        offs_list = load_list("offs_list", offs)
+        d_table_words = sb("d_table_words", [P, G], U32)
+        nc.sync.dma_start(d_table_words[:].bitcast(I32), d_words[0].rearrange("p n t -> p (n t)").bitcast(I32))
+        x_table_words = sb("x_table_words", [P, T], U32)
+        nc.sync.dma_start(x_table_words[:].bitcast(I32), x_words[0].rearrange("p n t -> p (n t)").bitcast(I32))
         n1_list = load_list("n1_list", n1)
         n2_list = load_list("n2_list", n2)
         cand_list = load_list("cand_list", cand)
         n3_list = load_list("n3_list", n3)
-        gs_sb = sb("gs_sb", [P, PACK], F32)
-        tau_sb = sb("tau_sb", [P, PACK], F32)
-        nc.gpsimd.dma_start(gs_sb[:], gs.rearrange("(p t) o -> p (t o)", t=PACK))
-        nc.gpsimd.dma_start(tau_sb[:], tau.rearrange("(p t) o -> p (t o)", t=PACK))
 
         s_rows = [sb(f"s_rows{t}", [P, WINDOW], F32) for t in range(PACK)]
         for t in range(PACK):
-            nc.vector.memset(s_rows[t][:, S:WINDOW], 0.0)
+            nc.gpsimd.memset(s_rows[t][:, S:WINDOW], 0.0)
 
         d_bytes = sb("d_bytes", [P, H], U8)
         nc.vector.tensor_copy(out=d_bytes[:], in_=d_table_bytes[:].indirect(k1_list[:]))
-        d_plane = sb("d_plane", [P, H], U8, tag="stationary_plane")
-        deal(d_plane, d_bytes)
-        for j in range(2):
-            nc.scalar.dma_start(d_plane[2 + j : P : 32, :].bitcast(I32), d_plane[16 + j : P : 32, :].bitcast(I32))
+        d_plane = sb("d_plane", [P, H], U8)
+        deal(d_plane, d_bytes, 16)
+        for j in range(1, 4):
+            nc.scalar.dma_start(d_plane[j:P:32, :].bitcast(I32), d_plane[8 * j : P : 32, :].bitcast(I32))
         d_picked = sb("d_picked", [P, H], U32)
         nc.vector.tensor_copy(out=d_picked[:], in_=d_table_words[:].indirect(k1_list[:]))
-        d_codes = sb("d_codes", [P, H], U32, tag="stationary_codes")
-        deal(d_codes, d_picked)
+        d_codes = sb("d_codes", [P, H], U32)
+        deal(d_codes, d_picked, 4)
 
         xq_codes = [sb(f"xq_codes{u}", [P, HALF], U32) for u in range(2)]
         xq_plane = [sb(f"xq_plane{u}", [P, HALF], U8) for u in range(2)]
@@ -94,73 +96,86 @@ def tile_picked_pqckgateegp_none_po_kernel(
             nc.vector.tensor_copy(out=xq_codes[u][:], in_=x_table_words[:].indirect(picks))
             nc.vector.tensor_copy(out=xq_plane[u][:], in_=x_table_bytes[:].indirect(picks))
 
+        tau_sb = sb("tau_sb", [P, PACK], F32, tag="d_picked")
+        nc.sync.dma_start(tau_sb[:], tau.rearrange("(p t) o -> p (t o)", t=PACK))
         neg_tau = sb("neg_tau", [P, PACK], F32)
-        nc.vector.tensor_scalar(neg_tau[:], tau_sb[:], -1.0, None, ALU.mult)
+        nc.gpsimd.tensor_scalar(neg_tau[:], tau_sb[:], -1.0, 0.0, ALU.mult, ALU.add)
 
-        h_rows = [sb(f"h_rows{t}", [P, S], F32) for t in range(PACK)]
-        h_banks = {}
-        for u in range(2):
-            for t in range(PACK):
-                cols = slice(t * P, (t + 1) * P)
-                h_banks[t, u] = psum.tile([P, HALF], F32, name=f"h_bank{t}_{u}", tag=f"bank{t}_{u}")
+        def first_product(t, name, halves):
+            rows = slice(t * P, (t + 1) * P)
+            bank = psum.tile([P, len(halves) * HALF], F32, name=name, tag=name)
+            for i, u in enumerate(halves):
                 nc.tensor.matmul_mx(
-                    out=h_banks[t, u][:],
-                    lhsT=d_codes[:, cols].bitcast(FP8X4),
-                    lhsT_scale=d_plane[:, cols],
+                    out=bank[:, i * HALF : (i + 1) * HALF],
+                    lhsT=d_codes[:, rows].bitcast(FP8X4),
+                    lhsT_scale=d_plane[:, rows],
                     rhs=xq_codes[u][:].bitcast(FP8X4),
                     rhs_scale=xq_plane[u][:],
                     start=True,
                     stop=True,
                 )
-        for t in range(PACK):
-            nc.scalar.activation(h_rows[t][:, 0:HALF], h_banks[t, 0][:], ACT.Copy, scale=0.0625)
+            return bank
 
+        left = [first_product(t, f"bank{t}", (0,)) for t in range(2)]
+        right = [first_product(t, f"right_bank{t}", (1,)) for t in range(2)]
+        whole = {t: first_product(t, f"bank{t}", (0, 1)) for t in range(2, PACK)}
+
+        h_rows, half_old, gate, ra = {}, {}, {}, {}
         ds_rows = [sb(f"ds_rows{t}", [P, S], F32) for t in range(PACK)]
-        half_old = [sb(f"half_old{t}", [P, W], F32) for t in range(PACK)]
-        pa = [sb(f"pa{t}", [P, W], F32) for t in range(PACK)]
-        gate = [sb(f"gate{t}", [P, W], F32) for t in range(PACK)]
-        ra = [sb(f"ra{t}", [P, W], F32) for t in range(PACK)]
 
-        def finish_h(t):
-            nc.vector.tensor_scalar(h_rows[t][:, HALF:S], h_banks[t, 1][:], 0.0625, None, ALU.mult)
+        def fetch_old(t, slot=None):
+            half_old[t] = sb(f"half_old{t}", [P, W], F32, tag=slot)
             nc.scalar.activation(half_old[t][:], h_rows[t][:].indirect(n1_list[:]), ACT.Copy, scale=0.5)
 
         def fetch_gate(t):
-            nc.vector.tensor_copy(out=pa[t][:], in_=h_rows[t][:].indirect(n2_list[:]))
-            nc.scalar.activation(gate[t][:], pa[t][:], ACT.Tanh, scale=0.5)
+            pa = sb(f"pa{t}", [P, W], F32)
+            gate[t] = sb(f"gate{t}", [P, W], F32)
+            nc.vector.tensor_copy(out=pa[:], in_=h_rows[t][:].indirect(n2_list[:]))
+            nc.scalar.activation(gate[t][:], pa[:], ACT.Tanh, scale=0.5)
 
         def gated(t):
-            nc.vector.tensor_copy(out=ds_rows[t][:], in_=h_rows[t][:])
+            ra[t] = sb(f"ra{t}", [P, W], F32)
             nc.vector.scalar_tensor_tensor(ra[t][:], gate[t][:], 1.0, half_old[t][:], ALU.add, ALU.mult)
 
         def put_back(t):
             nc.scalar.activation(ds_rows[t][:].indirect(n1_list[:]), ra[t][:], ACT.Copy)
 
-        finish_h(0)
-        fetch_gate(0)
-        finish_h(1)
+        for t in range(2):
+            h_rows[t] = sb(f"h_rows{t}", [P, S], F32)
+            nc.scalar.activation(h_rows[t][:, 0:HALF], left[t][:], ACT.Copy, scale=0.0625)
+        for t in range(2):
+            nc.vector.tensor_scalar(h_rows[t][:, HALF:S], right[t][:], 0.0625, None, ALU.mult)
+            fetch_old(t)
+        for t in range(2):
+            fetch_gate(t)
+        nc.vector.tensor_copy(out=ds_rows[0][:], in_=h_rows[0][:])
         gated(0)
         put_back(0)
-        fetch_gate(1)
+        for t, slot in ((2, "gate0"), (3, "half_old0")):
+            h_rows[t] = sb(f"h_rows{t}", [P, S], F32, tag=slot)
+            nc.vector.tensor_scalar(h_rows[t][:], whole[t][:], 0.0625, None, ALU.mult)
+        for t in range(1, PACK):
+            nc.sync.dma_start(ds_rows[t][:], h_rows[t][:])
         for t in range(2, PACK):
-            finish_h(t)
-        for t in range(2, PACK):
+            fetch_old(t)
             fetch_gate(t)
         for t in range(1, PACK):
             gated(t)
         for t in range(1, PACK):
             put_back(t)
 
-        cand_picked = sb("cand_picked", [P, C], U32, tag="stationary_codes")
-        cand_bytes = sb("cand_bytes", [P, C], U8, tag="stationary_plane")
+        gs_sb = sb("gs_sb", [P, PACK], F32, tag="gate1")
+        nc.sync.dma_start(gs_sb[:], gs.rearrange("(p t) o -> p (t o)", t=PACK))
+        cand_picked = sb("cand_picked", [P, C], U32, tag="half_old2")
+        cand_bytes = sb("cand_bytes", [P, C], U8, tag="gate2")
         cand_codes = sb("cand_codes", [P, C], U32)
         cand_plane = sb("cand_plane", [P, C], U8)
         nc.vector.tensor_copy(out=cand_picked[:], in_=x_table_words[:].indirect(cand_list[:]))
         nc.vector.tensor_copy(out=cand_bytes[:], in_=x_table_bytes[:].indirect(cand_list[:]))
-        deal(cand_codes, cand_picked)
-        deal(cand_plane, cand_bytes)
+        deal(cand_codes, cand_picked, 4)
+        deal(cand_plane, cand_bytes, 16)
 
-        z_bf = [sb(f"z_bf{u}", [P, HALF, PACK], BF16) for u in range(2)]
+        z_bf = [sb(f"z_bf{u}", [P, HALF, PACK], BF16, tag=("half_old2", "gate2")[u]) for u in range(2)]
         z_codes = [sb(f"z_codes{u}", [P, HALF], U32) for u in range(2)]
         z_plane = [sb(f"z_plane{u}", [P, HALF], U8) for u in range(2)]
         for t in range(PACK):
@@ -176,7 +191,7 @@ def tile_picked_pqckgateegp_none_po_kernel(
         bias = []
         for t in range(PACK):
             cols = slice(t * P, (t + 1) * P)
-            s_bank = psum.tile([P, S], F32, name=f"s_bank{t}", tag=f"bank{t}_0")
+            s_bank = psum.tile([P, S], F32, name=f"s_bank{t}", tag=f"bank{t}")
             for u in range(2):
                 nc.tensor.matmul_mx(
                     out=s_bank[:, u * HALF : (u + 1) * HALF],
@@ -192,65 +207,68 @@ def tile_picked_pqckgateegp_none_po_kernel(
             bias.append(sb(f"bias{t}", [P, 1], F32))
             nc.scalar.activation(bias[t][:], top[:], ACT.Copy, scale=neg_tau[:, t : t + 1])
 
-        entries = CHUNK * MEMBERS
         ea = []
         for g, (c, ts) in enumerate(GRANULES):
-            ea.append(sb(f"ea{g}", [P, len(ts) * entries], F32))
-            picks = n3_list[:, c * entries // 16 : (c + 1) * entries // 16]
+            start, width = CHUNKS[c]
+            ea.append(sb(f"ea{g}", [P, GRANULE * MEMBERS], F32))
             for i, t in enumerate(ts):
-                nc.scalar.activation(
-                    ea[g][:, i * entries : (i + 1) * entries],
-                    s_rows[t][:].indirect(picks),
-                    ACT.Exp,
-                    bias=bias[t][:],
-                    scale=tau_sb[:, t : t + 1],
-                )
+                for e in range(0, width * MEMBERS, PICKS):
+                    first = start * MEMBERS + e
+                    at = i * width * MEMBERS + e
+                    nc.scalar.activation(
+                        ea[g][:, at : at + PICKS],
+                        s_rows[t][:].indirect(n3_list[:, first // 16 : (first + PICKS) // 16]),
+                        ACT.Exp,
+                        bias=bias[t][:],
+                        scale=tau_sb[:, t : t + 1],
+                    )
 
-        out_chunks = [sb(f"out_chunk{c}", [P, PACK, CHUNK], F32) for c in range(S // CHUNK)]
+        out_chunks = [sb(f"out_chunk{c}", [P, PACK, width], F32) for c, (start, width) in enumerate(CHUNKS)]
+        out_bf = [sb(f"out_bf{c}", [P, width, PACK], BF16) for c, (start, width) in enumerate(CHUNKS)]
         out_rows = out_0.rearrange("(p t) j -> p t j", t=PACK)
         hi, lo, mx, mn, spread = {}, {}, {}, {}, {}
 
         def pairs(g, store, name, op):
-            n = len(GRANULES[g][1]) * CHUNK
-            store[g] = sb(f"{name}{g}", [P, n, 2], F32)
+            store[g] = sb(f"{name}{g}", [P, GRANULE, 2], F32)
             members = ea[g][:].rearrange("p (j m) -> p j m", m=MEMBERS)
             nc.vector.tensor_tensor(store[g][:], members[:, :, 0:2], members[:, :, 2:4], op)
 
         def fours(g, store, name, src, op):
-            n = len(GRANULES[g][1]) * CHUNK
-            store[g] = sb(f"{name}{g}", [P, n], F32)
+            store[g] = sb(f"{name}{g}", [P, GRANULE], F32)
             nc.vector.tensor_tensor(store[g][:], src[g][:, :, 0], src[g][:, :, 1], op)
 
         def difference(g):
-            n = len(GRANULES[g][1]) * CHUNK
-            spread[g] = sb(f"spread{g}", [P, n], F32)
+            spread[g] = sb(f"spread{g}", [P, GRANULE], F32)
             nc.vector.tensor_tensor(spread[g][:], mx[g][:], mn[g][:], ALU.subtract)
 
         def result(g):
             c, ts = GRANULES[g]
+            start, width = CHUNKS[c]
             for i, t in enumerate(ts):
                 nc.vector.scalar_tensor_tensor(
                     out_chunks[c][:, t, :],
-                    spread[g][:, i * CHUNK : (i + 1) * CHUNK],
+                    spread[g][:, i * width : (i + 1) * width],
                     3.0,
-                    s_rows[t][:, c * CHUNK : (c + 1) * CHUNK],
+                    s_rows[t][:, start : start + width],
                     ALU.mult,
                     ALU.mult,
                 )
             if ts[-1] == PACK - 1:
-                nc.sync.dma_start(out_rows[:, :, c * CHUNK : (c + 1) * CHUNK], out_chunks[c][:])
+                nc.sync.dma_start(out_rows[:, :, start : start + width], out_chunks[c][:])
 
         out_codes = sb("out_codes", [P, S], U32)
         out_plane = sb("out_plane", [P, S], U8)
-        out_bf = [sb(f"out_bf{c}", [P, CHUNK, PACK], BF16) for c in range(S // CHUNK)]
+        word_rows = out_1[0].rearrange("p n t -> p (n t)").bitcast(I32)
 
         def quantise(c):
-            cols = slice(c * CHUNK, (c + 1) * CHUNK)
+            start, width = CHUNKS[c]
+            cols = slice(start, start + width)
             nc.vector.quantize_mx(
                 out=out_codes[:, cols].bitcast(FP8X4),
                 scales=out_plane[:, cols],
                 in_=out_bf[c][:].rearrange("p j t -> p (j t)"),
             )
+            nc.sync.dma_start(word_rows[:, cols], out_codes[:, cols].bitcast(I32))
 
         last = len(GRANULES) - 1
         for g in range(len(GRANULES)):
@@ -262,19 +280,17 @@ def tile_picked_pqckgateegp_none_po_kernel(
                 result(g - 1)
             fours(g, mx, "mx", hi, ALU.max)
             fours(g, mn, "mn", lo, ALU.min)
-        last_chunk = S // CHUNK - 1
+        last_chunk = len(CHUNKS) - 1
         for c in range(last_chunk):
             nc.scalar.activation(out_bf[c][:], out_chunks[c][:].rearrange("p t j -> p j t"), ACT.Copy)
         quantise(0)
         difference(last)
         quantise(1)
         result(last)
-        quantise(2)
         nc.vector.tensor_copy(out=out_bf[last_chunk][:], in_=out_chunks[last_chunk][:].rearrange("p t j -> p j t"))
         quantise(last_chunk)
 
-        nc.sync.dma_start(out_1[0].rearrange("p n t -> p (n t)").bitcast(I32), out_codes[:].bitcast(I32))
         plane_rows = out_2[0].bitcast(I32)
         for q in range(4):
-            queue = nc.scalar if q % 2 == 0 else nc.sync
+            queue = nc.scalar if q < 3 else nc.sync
             queue.dma_start(plane_rows[4 * q : 4 * q + 4, :], out_plane[32 * q : 32 * q + 4, :].bitcast(I32))

from contextlib import ExitStack

import concourse.mybir as mybir

K, T, S, G, H, W, C = 512, 1024, 512, 2048, 512, 384, 512
FLOPS = 2 * K * H * S + 2 * K * C * S

F32 = mybir.dt.float32
BF16 = mybir.dt.bfloat16
I32 = mybir.dt.int32
U32 = mybir.dt.uint32
U16 = mybir.dt.uint16
U8 = mybir.dt.uint8
FP8X4 = mybir.dt.float8_e4m3fn_x4
ALU = mybir.AluOpType
ACT = mybir.ActivationFunctionType

P = 128
PACK = 4
MEMBERS = 4
HALF = S // 2
WINDOW = 1024
PICKS = 512
CHUNKS = [(0, 256), (256, 128), (384, 128)]
GRANULE = 256
GRANULES = [
    (c, tuple(range(t0, t0 + GRANULE // width)))
    for c, (start, width) in enumerate(CHUNKS)
    for t0 in range(0, PACK, GRANULE // width)
]


def tile_picked_pqckgateegp_none_po_kernel(
    tc, x_words, x_scales, d_words, d_scales, gs, tau, offs, k1, n1, n2, cand, n3, out_0, out_1, out_2
):
    nc = tc.nc
    with ExitStack() as ctx:
        pool = ctx.enter_context(tc.tile_pool(name="sbuf", bufs=1))
        psum = ctx.enter_context(tc.psum_pool(name="psum", bufs=1))

        def sb(name, shape, dtype, tag=None):
            return pool.tile(shape, dtype, name=name, tag=tag or name, align_bytes=64)

        def load_list(name, src):
            tile = sb(name, list(src.shape), U16)
            nc.sync.dma_start(tile[:], src)
            return tile

        def deal(dst, src, run):
            nc.vector.tensor_copy(
                out=dst[:].rearrange("p (t b i) -> p b t i", t=PACK, i=run),
                in_=src[:].rearrange("p (b i t) -> p b t i", t=PACK, i=run),
            )

        d_table_bytes = sb("d_table_bytes", [P, G], U8)
        x_table_bytes = sb("x_table_bytes", [P, T], U8)
        x_rows = x_scales[0].bitcast(I32)
        for q in range(4):
            nc.scalar.dma_start(
                x_table_bytes[32 * q : 32 * q + 32, :].bitcast(I32),
                x_rows[4 * q : 4 * q + 4, :].unsqueeze(0).to_broadcast([8, 4, T // 4]),
            )

        k1_list = load_list("k1_list", k1)
        d_rows = d_scales[0].bitcast(I32)
        nc.sync.dma_start(d_table_bytes[:].bitcast(I32), d_rows.unsqueeze(1).to_broadcast([16, 8, G // 4]))
        offs_list = load_list("offs_list", offs)
        d_table_words = sb("d_table_words", [P, G], U32)
        nc.sync.dma_start(d_table_words[:].bitcast(I32), d_words[0].rearrange("p n t -> p (n t)").bitcast(I32))
        x_table_words = sb("x_table_words", [P, T], U32)
        nc.sync.dma_start(x_table_words[:].bitcast(I32), x_words[0].rearrange("p n t -> p (n t)").bitcast(I32))
        n1_list = load_list("n1_list", n1)
        n2_list = load_list("n2_list", n2)
        cand_list = load_list("cand_list", cand)
        n3_list = load_list("n3_list", n3)

        s_rows = [sb(f"s_rows{t}", [P, WINDOW], F32) for t in range(PACK)]
        for t in range(PACK):
            nc.gpsimd.memset(s_rows[t][:, S:WINDOW], 0.0)

        d_bytes = sb("d_bytes", [P, H], U8)
        nc.vector.tensor_copy(out=d_bytes[:], in_=d_table_bytes[:].indirect(k1_list[:]))
        d_plane = sb("d_plane", [P, H], U8)
        deal(d_plane, d_bytes, 16)
        for j in range(1, 4):
            nc.scalar.dma_start(d_plane[j:P:32, :].bitcast(I32), d_plane[8 * j : P : 32, :].bitcast(I32))
        d_picked = sb("d_picked", [P, H], U32)
        nc.vector.tensor_copy(out=d_picked[:], in_=d_table_words[:].indirect(k1_list[:]))
        d_codes = sb("d_codes", [P, H], U32)
        deal(d_codes, d_picked, 4)

        xq_codes = [sb(f"xq_codes{u}", [P, HALF], U32) for u in range(2)]
        xq_plane = [sb(f"xq_plane{u}", [P, HALF], U8) for u in range(2)]
        for u in range(2):
            picks = offs_list[:, u * HALF // 16 : (u + 1) * HALF // 16]
            nc.vector.tensor_copy(out=xq_codes[u][:], in_=x_table_words[:].indirect(picks))
            nc.vector.tensor_copy(out=xq_plane[u][:], in_=x_table_bytes[:].indirect(picks))

        tau_sb = sb("tau_sb", [P, PACK], F32, tag="d_picked")
        nc.sync.dma_start(tau_sb[:], tau.rearrange("(p t) o -> p (t o)", t=PACK))
        neg_tau = sb("neg_tau", [P, PACK], F32)
        nc.gpsimd.tensor_scalar(neg_tau[:], tau_sb[:], -1.0, 0.0, ALU.mult, ALU.add)

        def first_product(t, name, halves):
            rows = slice(t * P, (t + 1) * P)
            bank = psum.tile([P, len(halves) * HALF], F32, name=name, tag=name)
            for i, u in enumerate(halves):
                nc.tensor.matmul_mx(
                    out=bank[:, i * HALF : (i + 1) * HALF],
                    lhsT=d_codes[:, rows].bitcast(FP8X4),
                    lhsT_scale=d_plane[:, rows],
                    rhs=xq_codes[u][:].bitcast(FP8X4),
                    rhs_scale=xq_plane[u][:],
                    start=True,
                    stop=True,
                )
            return bank

        left = [first_product(t, f"bank{t}", (0,)) for t in range(2)]
        right = [first_product(t, f"right_bank{t}", (1,)) for t in range(2)]
        whole = {t: first_product(t, f"bank{t}", (0, 1)) for t in range(2, PACK)}

        h_rows, half_old, gate, ra = {}, {}, {}, {}
        ds_rows = [sb(f"ds_rows{t}", [P, S], F32) for t in range(PACK)]

        def fetch_old(t, slot=None):
            half_old[t] = sb(f"half_old{t}", [P, W], F32, tag=slot)
            nc.scalar.activation(half_old[t][:], h_rows[t][:].indirect(n1_list[:]), ACT.Copy, scale=0.5)

        def fetch_gate(t):
            pa = sb(f"pa{t}", [P, W], F32)
            gate[t] = sb(f"gate{t}", [P, W], F32)
            nc.vector.tensor_copy(out=pa[:], in_=h_rows[t][:].indirect(n2_list[:]))
            nc.scalar.activation(gate[t][:], pa[:], ACT.Tanh, scale=0.5)

        def gated(t):
            ra[t] = sb(f"ra{t}", [P, W], F32)
            nc.vector.scalar_tensor_tensor(ra[t][:], gate[t][:], 1.0, half_old[t][:], ALU.add, ALU.mult)

        def put_back(t):
            nc.scalar.activation(ds_rows[t][:].indirect(n1_list[:]), ra[t][:], ACT.Copy)

        for t in range(2):
            h_rows[t] = sb(f"h_rows{t}", [P, S], F32)
            nc.scalar.activation(h_rows[t][:, 0:HALF], left[t][:], ACT.Copy, scale=0.0625)
        for t in range(2):
            nc.vector.tensor_scalar(h_rows[t][:, HALF:S], right[t][:], 0.0625, None, ALU.mult)
            fetch_old(t)
        for t in range(2):
            fetch_gate(t)
        nc.vector.tensor_copy(out=ds_rows[0][:], in_=h_rows[0][:])
        gated(0)
        put_back(0)
        for t, slot in ((2, "gate0"), (3, "half_old0")):
            h_rows[t] = sb(f"h_rows{t}", [P, S], F32, tag=slot)
            nc.vector.tensor_scalar(h_rows[t][:], whole[t][:], 0.0625, None, ALU.mult)
        for t in range(1, PACK):
            nc.sync.dma_start(ds_rows[t][:], h_rows[t][:])
        for t in range(2, PACK):
            fetch_old(t)
            fetch_gate(t)
        for t in range(1, PACK):
            gated(t)
        for t in range(1, PACK):
            put_back(t)

        gs_sb = sb("gs_sb", [P, PACK], F32, tag="gate1")
        nc.sync.dma_start(gs_sb[:], gs.rearrange("(p t) o -> p (t o)", t=PACK))
        cand_picked = sb("cand_picked", [P, C], U32, tag="half_old2")
        cand_bytes = sb("cand_bytes", [P, C], U8, tag="gate2")
        cand_codes = sb("cand_codes", [P, C], U32)
        cand_plane = sb("cand_plane", [P, C], U8)
        nc.vector.tensor_copy(out=cand_picked[:], in_=x_table_words[:].indirect(cand_list[:]))
        nc.vector.tensor_copy(out=cand_bytes[:], in_=x_table_bytes[:].indirect(cand_list[:]))
        deal(cand_codes, cand_picked, 4)
        deal(cand_plane, cand_bytes, 16)

        z_bf = [sb(f"z_bf{u}", [P, HALF, PACK], BF16, tag=("half_old2", "gate2")[u]) for u in range(2)]
        z_codes = [sb(f"z_codes{u}", [P, HALF], U32) for u in range(2)]
        z_plane = [sb(f"z_plane{u}", [P, HALF], U8) for u in range(2)]
        for t in range(PACK):
            for u in range(2):
                nc.vector.tensor_scalar(
                    z_bf[u][:, :, t], ds_rows[t][:, u * HALF : (u + 1) * HALF], gs_sb[:, t : t + 1], None, ALU.mult
                )
        for u in range(2):
            nc.vector.quantize_mx(
                out=z_codes[u][:].bitcast(FP8X4), scales=z_plane[u][:], in_=z_bf[u][:].rearrange("p j t -> p (j t)")
            )

        bias = []
        for t in range(PACK):
            cols = slice(t * P, (t + 1) * P)
            s_bank = psum.tile([P, S], F32, name=f"s_bank{t}", tag=f"bank{t}")
            for u in range(2):
                nc.tensor.matmul_mx(
                    out=s_bank[:, u * HALF : (u + 1) * HALF],
                    lhsT=cand_codes[:, cols].bitcast(FP8X4),
                    lhsT_scale=cand_plane[:, cols],
                    rhs=z_codes[u][:].bitcast(FP8X4),
                    rhs_scale=z_plane[u][:],
                    start=True,
                    stop=True,
                )
            top = sb(f"top{t}", [P, 1], F32)
            nc.vector.tensor_scalar(s_rows[t][:, 0:S], s_bank[:], 0.0625, None, ALU.mult, ALU.max, accum_out=top[:])
            bias.append(sb(f"bias{t}", [P, 1], F32))
            nc.scalar.activation(bias[t][:], top[:], ACT.Copy, scale=neg_tau[:, t : t + 1])

        ea = []
        for g, (c, ts) in enumerate(GRANULES):
            start, width = CHUNKS[c]
            ea.append(sb(f"ea{g}", [P, GRANULE * MEMBERS], F32))
            for i, t in enumerate(ts):
                for e in range(0, width * MEMBERS, PICKS):
                    first = start * MEMBERS + e
                    at = i * width * MEMBERS + e
                    nc.scalar.activation(
                        ea[g][:, at : at + PICKS],
                        s_rows[t][:].indirect(n3_list[:, first // 16 : (first + PICKS) // 16]),
                        ACT.Exp,
                        bias=bias[t][:],
                        scale=tau_sb[:, t : t + 1],
                    )

        out_chunks = [sb(f"out_chunk{c}", [P, PACK, width], F32) for c, (start, width) in enumerate(CHUNKS)]
        out_bf = [sb(f"out_bf{c}", [P, width, PACK], BF16) for c, (start, width) in enumerate(CHUNKS)]
        out_rows = out_0.rearrange("(p t) j -> p t j", t=PACK)
        hi, lo, mx, mn, spread = {}, {}, {}, {}, {}

        def pairs(g, store, name, op):
            store[g] = sb(f"{name}{g}", [P, GRANULE, 2], F32)
            members = ea[g][:].rearrange("p (j m) -> p j m", m=MEMBERS)
            nc.vector.tensor_tensor(store[g][:], members[:, :, 0:2], members[:, :, 2:4], op)

        def fours(g, store, name, src, op):
            store[g] = sb(f"{name}{g}", [P, GRANULE], F32)
            nc.vector.tensor_tensor(store[g][:], src[g][:, :, 0], src[g][:, :, 1], op)

        def difference(g):
            spread[g] = sb(f"spread{g}", [P, GRANULE], F32)
            nc.vector.tensor_tensor(spread[g][:], mx[g][:], mn[g][:], ALU.subtract)

        def result(g):
            c, ts = GRANULES[g]
            start, width = CHUNKS[c]
            for i, t in enumerate(ts):
                nc.vector.scalar_tensor_tensor(
                    out_chunks[c][:, t, :],
                    spread[g][:, i * width : (i + 1) * width],
                    3.0,
                    s_rows[t][:, start : start + width],
                    ALU.mult,
                    ALU.mult,
                )
            if ts[-1] == PACK - 1:
                nc.sync.dma_start(out_rows[:, :, start : start + width], out_chunks[c][:])

        out_codes = sb("out_codes", [P, S], U32)
        out_plane = sb("out_plane", [P, S], U8)
        word_rows = out_1[0].rearrange("p n t -> p (n t)").bitcast(I32)

        def quantise(c):
            start, width = CHUNKS[c]
            cols = slice(start, start + width)
            nc.vector.quantize_mx(
                out=out_codes[:, cols].bitcast(FP8X4),
                scales=out_plane[:, cols],
                in_=out_bf[c][:].rearrange("p j t -> p (j t)"),
            )
            nc.sync.dma_start(word_rows[:, cols], out_codes[:, cols].bitcast(I32))

        last = len(GRANULES) - 1
        for g in range(len(GRANULES)):
            pairs(g, hi, "hi", ALU.max)
            if g > 0:
                difference(g - 1)
            pairs(g, lo, "lo", ALU.min)
            if g > 0:
                result(g - 1)
            fours(g, mx, "mx", hi, ALU.max)
            fours(g, mn, "mn", lo, ALU.min)
        last_chunk = len(CHUNKS) - 1
        for c in range(last_chunk):
            nc.scalar.activation(out_bf[c][:], out_chunks[c][:].rearrange("p t j -> p j t"), ACT.Copy)
        quantise(0)
        difference(last)
        quantise(1)
        result(last)
        nc.vector.tensor_copy(out=out_bf[last_chunk][:], in_=out_chunks[last_chunk][:].rearrange("p t j -> p j t"))
        quantise(last_chunk)

        plane_rows = out_2[0].bitcast(I32)
        for q in range(4):
            queue = nc.scalar if q < 3 else nc.sync
            queue.dma_start(plane_rows[4 * q : 4 * q + 4, :], out_plane[32 * q : 32 * q + 4, :].bitcast(I32))
